import numpy as np, ml_dtypes
CORES = [1,2,5,7,57,58,61,63,73,74,77,79]
N = 12
KB, QP = 1, 256
ROOT = 1
def setup_inputs(rng):
    q = rng.standard_normal((N, 128, QP), dtype=np.float32) / 4; k = rng.standard_normal((N, 128, KB * 128), dtype=np.float32)
    a = 2 * np.pi * rng.random((N, QP)); s = 400 * rng.random((N, QP)) ** 1.5; q[:, 0, :] = s * np.cos(a); q[:, 1, :] = s * np.sin(a); q[:, 2, :] = 150 * rng.standard_normal((N, QP)); k[:, 2, :] = 1 + k[:, 2, :] / 50
    a = (2 * np.pi * rng.random() + np.pi / 2 * (rng.permutation(N).reshape(N, 1, 1) + 0.5) / N - 0.5 + (np.arange(KB).reshape(1, KB, 1) + rng.random((N, KB, 128))) / KB).reshape(N, KB * 128); k[:, 0, :] = np.cos(a); k[:, 1, :] = np.sin(a)
    for t in range(0, QP, 2):
        j, i = (t // 2) % N, rng.integers(KB * 128); q[ROOT, :2, t] = s[ROOT, t] * k[j, :2, i]; q[ROOT, 3:, t] += k[j, 3:, i] / 8
    return {"q": q.astype(ml_dtypes.bfloat16), "k": k.astype(ml_dtypes.bfloat16), "v": rng.standard_normal((N, 128, KB * 128), dtype=np.float32).astype(ml_dtypes.bfloat16)}
def setup_inputs_big(rng):
    d = setup_inputs(rng)
    for k in ("v",): d[k] = (d[k].astype(np.float32) * 1048576.0).astype(d[k].dtype)
    return d
def setup_inputs_small(rng):
    d = setup_inputs(rng)
    for k in ("v",): d[k] = (d[k].astype(np.float32) * (1 / 1048576.0)).astype(d[k].dtype)
    return d
def reference(q, k, v):
    Q, K, V = q.astype(np.float64), k.astype(np.float64), v.astype(np.float64)
    y = np.full((N, QP, 128), np.nan)
    for r in [ROOT]:
        js = list(range(N))
        S = np.concatenate([K[j].T @ Q[r] for j in js], axis=0)
        P = np.exp(S - S.max(axis=0)); P = P / P.sum(axis=0)
        y[r] = P.T @ np.concatenate([V[j][:, 128 * b:128 * b + 128] for j in js for b in range(KB)], axis=0)
    return {"y": y.astype(ml_dtypes.bfloat16)}

@@ -1,0 +1,286 @@
+from concourse.mybir import AluOpType, AxisListType, ActivationFunctionType
+
+NR = 12
+NG = 4
+
+SCRATCH = {
+    "kd": ("dram", [128, 128], "bfloat16"),
+    "vd": ("dram", [128, 128], "bfloat16"),
+    "rk": ("dram", [128, 128], "bfloat16"),
+    "rv": ("dram", [128, 128], "bfloat16"),
+    "qs": ("sbuf", [128, 256], "bfloat16"),
+    "Kall": ("sbuf", [128, NR * 128], "bfloat16"),
+    "Vall": ("sbuf", [128, NR * 128], "bfloat16"),
+    "ones": ("sbuf", [128, 128], "bfloat16"),
+    "ident": ("sbuf", [128, 128], "bfloat16"),
+    "P": ("sbuf", [128, 2 * NR * 128], "bfloat16"),
+    "PT": ("sbuf", [128, 2 * NR * 128], "bfloat16"),
+    "st": ("sbuf", [128, 128], "float32"),
+    "acc": ("sbuf", [128, 256], "float32"),
+    "ysb": ("sbuf", [128, 256], "bfloat16"),
+    "S0": ("psum", [128, 512], "float32"),
+    "S1": ("psum", [128, 512], "float32"),
+    "S2": ("psum", [128, 512], "float32"),
+    "S3": ("psum", [128, 512], "float32"),
+    "TA": ("psum", [128, 1024], "bfloat16"),
+    "TB": ("psum", [128, 1024], "bfloat16"),
+    "O0": ("psum", [128, 512], "float32"),
+    "O1": ("psum", [128, 512], "float32"),
+}
+SEMAPHORES = (["ldk", "ldv", "rka", "rva", "sent", "lq", "yd0", "yd1", "te", "ve", "se", "ge"]
+              + ["ak%d" % i for i in range(NG)] + ["av%d" % i for i in range(NG)])
+
+
+def _bits(m):
+    return bin(m).count("1")
+
+
+def _lowest(m, n):
+    out, b = 0, 1
+    while n > 0:
+        if m & b:
+            out |= b
+            n -= 1
+        b <<= 1
+    return out
+
+
+def _plan(T, topo):
+    cores = list(T.cores)
+    root = cores[T.root]
+    near = [r for r, c in enumerate(cores) if c != root and topo.chip(c) == topo.chip(root)]
+    far = [r for r, c in enumerate(cores) if topo.chip(c) != topo.chip(root)]
+    direct = [r for r in far if topo.may_write(cores[r], root)]
+    passed = [r for r in far if not topo.may_write(cores[r], root)]
+    via = {}
+    for r in passed:
+        c = cores[r]
+        cand = [d for d in direct if topo.chip(cores[d]) == topo.chip(c)]
+        same = [d for d in cand if topo.die(cores[d]) == topo.die(c)]
+        cand = same + [d for d in cand if d not in same]
+        free = [d for d in cand if d not in via.values()]
+        via[r] = (free or cand)[0]
+    groups = [[T.root], near, direct, passed]
+    slot = {}
+    for gi, grp in enumerate(groups):
+        for r in grp:
+            slot[r] = (gi, len(slot))
+    return cores, root, groups, slot, via
+
+
+def _send(g, T, topo, src, dst, out_ap, in_ap, rsem, n_eng):
+    rid, pid, _ = topo.addr(dst)
+    m = topo.mask(src, dst)
+    m = _lowest(m, min(n_eng, _bits(m)))
+    g.remote_dma(out_ap=out_ap, in_ap=in_ap, remote_sem=rsem, local_sem=T.sem.sent, pid=pid, routing_id=rid,
+                 dma_engine_mask=m)
+    return _bits(m)
+
+
+NE = 8
+
+
+def _sender(g, core, T, topo, rank, plan):
+    cores, root, groups, slot, via = plan
+    g.sync.dma_start(T.kd[:, :], T.k[:, :]).then_inc(T.sem.ldk, 16)
+    g.scalar.dma_start(T.vd[:, :], T.v[:, :]).then_inc(T.sem.ldv, 16)
+    sent = 0
+    if rank in via:
+        dst = cores[via[rank]]
+        g.wait_ge(T.sem.ldk, 16)
+        sent += _send(g, T, topo, core, dst, T.rk[:, :], T.kd[:, :], T.sem.rka, NE)
+        g.wait_ge(T.sem.ldv, 16)
+        sent += _send(g, T, topo, core, dst, T.rv[:, :], T.vd[:, :], T.sem.rva, NE)
+    else:
+        gi, s = slot[rank]
+        g.wait_ge(T.sem.ldk, 16)
+        sent += _send(g, T, topo, core, root, T.Kall[:, s * 128:(s + 1) * 128], T.kd[:, :], T.sem["ak%d" % gi], NE)
+        g.wait_ge(T.sem.ldv, 16)
+        sent += _send(g, T, topo, core, root, T.Vall[:, s * 128:(s + 1) * 128], T.vd[:, :], T.sem["av%d" % gi], NE)
+        for r in [r for r in via if via[r] == rank]:
+            gi, s = slot[r]
+            n_in = _bits(_lowest(topo.mask(cores[r], core), NE))
+            g.wait_ge(T.sem.rka, n_in)
+            sent += _send(g, T, topo, core, root, T.Kall[:, s * 128:(s + 1) * 128], T.rk[:, :], T.sem["ak%d" % gi], NE)
+            g.wait_ge(T.sem.rva, n_in)
+            sent += _send(g, T, topo, core, root, T.Vall[:, s * 128:(s + 1) * 128], T.rv[:, :], T.sem["av%d" % gi], NE)
+    g.wait_ge(T.sem.sent, sent)
+
+
+def _root(g, core, T, topo, plan):
+    cores, root, groups, slot, via = plan
+    te, ve, se = g.tensor, g.vector, g.scalar
+    Exp, Copy = ActivationFunctionType.Exp, ActivationFunctionType.Copy
+    cnt = {"te": 0, "ve": 0, "se": 0, "ge": 0}
+    seen = {}
+    queues = {"te": te, "ve": ve, "se": se, "ge": g, "sy": g.sync}
+
+    def post(ins, e):
+        cnt[e] += 1
+        ins.then_inc(T.sem[e], 1)
+        return (e, cnt[e])
+
+    def need(q, tok):
+        if tok is None:
+            return
+        e, n = tok
+        if seen.get((q, e), 0) >= n:
+            return
+        seen[(q, e)] = n
+        queues[q].wait_ge(T.sem[e], n)
+
+    ncol = [0]
+
+    def cols(n=1):
+        c = ncol[0]
+        ncol[0] += n
+        return T.st[:, c:c + n]
+
+    g.sync.dma_start(T.qs[:, :], T.q[:, :]).then_inc(T.sem.lq, 16)
+    g.scalar.dma_start(T.Kall[:, 0:128], T.k[:, :]).then_inc(T.sem.ak0, 16)
+    g.sync.dma_start(T.Vall[:, 0:128], T.v[:, :]).then_inc(T.sem.av0, 16)
+    need("ge", post(ve.memset(T.ones[:, :], 1.0), "ve"))
+    t_id = post(g.affine_select(T.ident[:, :], T.ones[:, :], [[-1, 128]], AluOpType.is_equal, 0.0, 0, 1), "ge")
+
+    def arrive(gi):
+        if gi == 0:
+            return 16
+        tot = 0
+        for r in groups[gi]:
+            src = cores[via[r]] if r in via else cores[r]
+            tot += _bits(_lowest(topo.mask(src, root), NE))
+        return tot
+
+    Sb = [T.S0, T.S1, T.S2, T.S3]
+    Tb = [T.TA, T.TB]
+    Ob = [T.O0, T.O1]
+    last = len(groups) - 1
+    t_exp_last = {}
+    t_copy = []
+    t_acc = {}
+    negM = {}
+    lacc = {}
+    te.wait_ge(T.sem.lq, 16)
+    for gi, grp in enumerate(groups):
+        n = len(grp)
+        s0 = slot[grp[0]][1]
+        te.wait_ge(T.sem["ak%d" % gi], arrive(gi))
+        t_S = {}
+        for h in (0, 1):
+            need("te", t_exp_last.get((gi - 2, h)))
+            t_S[h] = post(te.matmul(Sb[(gi % 2) * 2 + h][:, 0:128 * n], T.qs[:, h * 128:(h + 1) * 128],
+                                    T.Kall[:, s0 * 128:(s0 + n) * 128], True, True), "te")
+        t_M = {}
+        for h in (0, 1):
+            need("ve", t_S[h])
+            nm = cols()
+            t = post(ve.tensor_reduce(nm, Sb[(gi % 2) * 2 + h][:, 0:128 * n], AxisListType.X, AluOpType.max,
+                                      negate=True), "ve")
+            if gi > 0:
+                need("ve", t)
+                nM = cols()
+                t = post(ve.tensor_tensor(nM, negM[(gi - 1, h)], nm, AluOpType.min), "ve")
+                nm = nM
+            negM[(gi, h)] = nm
+            t_M[h] = t
+        t_exp = {}
+        lblk = {}
+        for h in (0, 1):
+            need("se", t_M[h])
+            lblk[h] = cols(n)
+            for i in range(n):
+                b = (h * NR + s0 + i) * 128
+                t_exp[(h, i)] = post(se.activation(T.P[:, b:b + 128], Sb[(gi % 2) * 2 + h][:, i * 128:(i + 1) * 128],
+                                                   Exp, bias=negM[(gi, h)], scale=1.0,
+                                                   accum_out=lblk[h][:, i:i + 1]), "se")
+            t_exp_last[(gi, h)] = t_exp[(h, n - 1)]
+        t_cp_last = {}
+        lsum = {}
+        t_ls = {}
+        for h in (0, 1):
+            for i in range(n):
+                b = (h * NR + s0 + i) * 128
+                k = len(t_copy)
+                need("te", t_id)
+                need("te", t_exp[(h, i)])
+                if k >= 2:
+                    need("te", t_copy[k - 2])
+                t = post(te.transpose(Tb[k % 2][:, 0:128], T.P[:, b:b + 128], T.ident[:, :]), "te")
+                need("ve", t)
+                t_copy.append(post(ve.tensor_copy(T.PT[:, b:b + 128], Tb[k % 2][:, 0:128]), "ve"))
+            t_cp_last[h] = t_copy[-1]
+            if n > 1:
+                need("ve", t_exp[(h, n - 1)])
+                lsum[h] = cols()
+                t_ls[h] = post(ve.tensor_reduce(lsum[h], lblk[h], AxisListType.X, AluOpType.add), "ve")
+            else:
+                lsum[h] = lblk[h]
+                t_ls[h] = t_exp[(h, 0)]
+        t_a, a, t_sc = {}, {}, {}
+        if gi > 0:
+            for h in (0, 1):
+                a[h] = cols()
+                t_a[h] = post(se.activation(a[h], negM[(gi - 1, h)], Exp, bias=negM[(gi, h)], scale=-1.0), "se")
+            for h in (0, 1):
+                need("se", t_a[h])
+                need("se", t_acc[(gi - 1, h)])
+                t_sc[h] = post(se.activation(T.acc[:, h * 128:(h + 1) * 128], T.acc[:, h * 128:(h + 1) * 128], Copy,
+                                             scale=a[h]), "se")
+        rc, t_r = {}, {}
+        for h in (0, 1):
+            if gi == 0:
+                lacc[(gi, h)] = lsum[h]
+                t_l = t_ls[h]
+            else:
+                need("ve", t_a[h])
+                need("ve", t_ls[h])
+                lacc[(gi, h)] = cols()
+                t_l = post(ve.tensor_scalar(lacc[(gi, h)], lacc[(gi - 1, h)], a[h], lsum[h], AluOpType.mult,
+                                            AluOpType.add), "ve")
+            if gi == 0:
+                need("ve", t_l)
+            if gi == last:
+                need("ve", t_l)
+                rc[h] = cols()
+                t_r[h] = post(ve.reciprocal(rc[h], lacc[(gi, h)]), "ve")
+        te.wait_ge(T.sem["av%d" % gi], arrive(gi))
+        t_PV = {}
+        for h in (0, 1):
+            need("te", t_cp_last[h])
+            need("te", t_acc.get((gi - 1, h)))
+            for i in range(n):
+                b = (h * NR + s0 + i) * 128
+                ins = te.matmul(Ob[h][:, 0:128], T.PT[:, b:b + 128], T.Vall[:, (s0 + i) * 128:(s0 + i + 1) * 128],
+                                i == 0, i == n - 1)
+            t_PV[h] = post(ins, "te")
+        for h in (0, 1):
+            A = T.acc[:, h * 128:(h + 1) * 128]
+            need("ve", t_PV[h])
+            if gi == 0:
+                t_acc[(gi, h)] = post(ve.tensor_copy(A, Ob[h][:, 0:128]), "ve")
+            else:
+                need("ve", t_sc[h])
+                t_acc[(gi, h)] = post(ve.tensor_tensor(A, Ob[h][:, 0:128], A, AluOpType.add), "ve")
+            if gi == last:
+                need("ve", t_acc[(gi, h)])
+                need("ve", t_r[h])
+                t_y = post(ve.tensor_scalar(T.ysb[:, h * 128:(h + 1) * 128], A, rc[h], None, AluOpType.mult), "ve")
+                q = "sy" if h == 0 else "se"
+                need(q, t_y)
+                queues[q].dma_start(T.y[h * 128:(h + 1) * 128, :], T.ysb[:, h * 128:(h + 1) * 128]).then_inc(
+                    T.sem["yd%d" % h], 16)
+    for e in ("te", "ve", "se", "ge"):
+        g.wait_ge(T.sem[e], cnt[e])
+    g.wait_ge(T.sem.yd0, 16)
+    g.wait_ge(T.sem.yd1, 16)
+
+
+def rank_program(g, core, T, topo):
+    rank = T.rank_of(core)
+    if rank is None:
+        return
+    plan = _plan(T, topo)
+    if rank == T.root:
+        _root(g, core, T, topo, plan)
+    else:
+        _sender(g, core, T, topo, rank, plan)

@@ -2,6 +2,7 @@ from concourse.mybir import AluOpType, AxisListType, ActivationFunctionType
 
 NR = 12
 NG = 4
+AHEAD = (1, 2)
 
 SCRATCH = {
     "kd": ("dram", [128, 128], "bfloat16"),
@@ -155,22 +156,20 @@ def _root(g, core, T, topo, plan):
     Tb = [T.TA, T.TB]
     Ob = [T.O0, T.O1]
     last = len(groups) - 1
-    t_exp_last = {}
-    t_copy = []
-    t_acc = {}
-    negM = {}
-    lacc = {}
+    t_exp, t_cp, t_acc, t_a = {}, {}, {}, {}
+    negM, lacc, lblk, a = {}, {}, {}, {}
     te.wait_ge(T.sem.lq, 16)
-    for gi, grp in enumerate(groups):
-        n = len(grp)
-        s0 = slot[grp[0]][1]
+
+    def stage_a(gi):
+        n = len(groups[gi])
+        s0 = slot[groups[gi][0]][1]
         te.wait_ge(T.sem["ak%d" % gi], arrive(gi))
-        t_S = {}
+        t_S, t_M = {}, {}
         for h in (0, 1):
-            need("te", t_exp_last.get((gi - 2, h)))
+            if gi >= 2:
+                need("te", t_exp[(gi - 2, h, len(groups[gi - 2]) - 1)])
             t_S[h] = post(te.matmul(Sb[(gi % 2) * 2 + h][:, 0:128 * n], T.qs[:, h * 128:(h + 1) * 128],
                                     T.Kall[:, s0 * 128:(s0 + n) * 128], True, True), "te")
-        t_M = {}
         for h in (0, 1):
             need("ve", t_S[h])
             nm = cols()
@@ -183,70 +182,63 @@ def _root(g, core, T, topo, plan):
                 nm = nM
             negM[(gi, h)] = nm
             t_M[h] = t
-        t_exp = {}
-        lblk = {}
         for h in (0, 1):
             need("se", t_M[h])
-            lblk[h] = cols(n)
+            lblk[(gi, h)] = cols(n)
             for i in range(n):
                 b = (h * NR + s0 + i) * 128
-                t_exp[(h, i)] = post(se.activation(T.P[:, b:b + 128], Sb[(gi % 2) * 2 + h][:, i * 128:(i + 1) * 128],
-                                                   Exp, bias=negM[(gi, h)], scale=1.0,
-                                                   accum_out=lblk[h][:, i:i + 1]), "se")
-            t_exp_last[(gi, h)] = t_exp[(h, n - 1)]
-        t_cp_last = {}
-        lsum = {}
-        t_ls = {}
-        for h in (0, 1):
-            for i in range(n):
-                b = (h * NR + s0 + i) * 128
-                k = len(t_copy)
-                need("te", t_id)
-                need("te", t_exp[(h, i)])
-                if k >= 2:
-                    need("te", t_copy[k - 2])
-                t = post(te.transpose(Tb[k % 2][:, 0:128], T.P[:, b:b + 128], T.ident[:, :]), "te")
-                need("ve", t)
-                t_copy.append(post(ve.tensor_copy(T.PT[:, b:b + 128], Tb[k % 2][:, 0:128]), "ve"))
-            t_cp_last[h] = t_copy[-1]
-            if n > 1:
-                need("ve", t_exp[(h, n - 1)])
-                lsum[h] = cols()
-                t_ls[h] = post(ve.tensor_reduce(lsum[h], lblk[h], AxisListType.X, AluOpType.add), "ve")
-            else:
-                lsum[h] = lblk[h]
-                t_ls[h] = t_exp[(h, 0)]
-        t_a, a, t_sc = {}, {}, {}
+                t_exp[(gi, h, i)] = post(se.activation(T.P[:, b:b + 128],
+                                                       Sb[(gi % 2) * 2 + h][:, i * 128:(i + 1) * 128],
+                                                       Exp, bias=negM[(gi, h)], scale=1.0,
+                                                       accum_out=lblk[(gi, h)][:, i:i + 1]), "se")
         if gi > 0:
             for h in (0, 1):
-                a[h] = cols()
-                t_a[h] = post(se.activation(a[h], negM[(gi - 1, h)], Exp, bias=negM[(gi, h)], scale=-1.0), "se")
+                a[(gi, h)] = cols()
+                t_a[(gi, h)] = post(se.activation(a[(gi, h)], negM[(gi - 1, h)], Exp, bias=negM[(gi, h)],
+                                                  scale=-1.0), "se")
+
+    def stage_b(gi):
+        n = len(groups[gi])
+        s0 = slot[groups[gi][0]][1]
+        rc, t_r, t_sc, t_PV = {}, {}, {}, {}
+        if gi > 0:
             for h in (0, 1):
-                need("se", t_a[h])
+                need("se", t_a[(gi, h)])
                 need("se", t_acc[(gi - 1, h)])
                 t_sc[h] = post(se.activation(T.acc[:, h * 128:(h + 1) * 128], T.acc[:, h * 128:(h + 1) * 128], Copy,
-                                             scale=a[h]), "se")
-        rc, t_r = {}, {}
+                                             scale=a[(gi, h)]), "se")
         for h in (0, 1):
-            if gi == 0:
-                lacc[(gi, h)] = lsum[h]
-                t_l = t_ls[h]
+            b0 = (h * NR + s0) * 128
+            need("te", t_id)
+            need("te", t_cp.get((gi - 1, h)))
+            for i in range(n):
+                need("te", t_exp[(gi, h, i)])
+                t = post(te.transpose(Tb[h][:, i * 128:(i + 1) * 128], T.P[:, b0 + i * 128:b0 + (i + 1) * 128],
+                                      T.ident[:, :]), "te")
+            need("ve", t)
+            t_cp[(gi, h)] = post(ve.tensor_copy(T.PT[:, b0:b0 + n * 128], Tb[h][:, 0:n * 128]), "ve")
+            need("ve", t_exp[(gi, h, n - 1)])
+            if n > 1:
+                ls = cols()
+                t_l = post(ve.tensor_reduce(ls, lblk[(gi, h)], AxisListType.X, AluOpType.add), "ve")
             else:
-                need("ve", t_a[h])
-                need("ve", t_ls[h])
-                lacc[(gi, h)] = cols()
-                t_l = post(ve.tensor_scalar(lacc[(gi, h)], lacc[(gi - 1, h)], a[h], lsum[h], AluOpType.mult,
-                                            AluOpType.add), "ve")
+                ls = lblk[(gi, h)]
+                t_l = None
             if gi == 0:
+                lacc[(gi, h)] = ls
+            else:
+                need("ve", t_a[(gi, h)])
                 need("ve", t_l)
+                lacc[(gi, h)] = cols()
+                t_l = post(ve.tensor_scalar(lacc[(gi, h)], lacc[(gi - 1, h)], a[(gi, h)], ls, AluOpType.mult,
+                                            AluOpType.add), "ve")
             if gi == last:
                 need("ve", t_l)
                 rc[h] = cols()
                 t_r[h] = post(ve.reciprocal(rc[h], lacc[(gi, h)]), "ve")
         te.wait_ge(T.sem["av%d" % gi], arrive(gi))
-        t_PV = {}
         for h in (0, 1):
-            need("te", t_cp_last[h])
+            need("te", t_cp[(gi, h)])
             need("te", t_acc.get((gi - 1, h)))
             for i in range(n):
                 b = (h * NR + s0 + i) * 128
@@ -269,6 +261,14 @@ def _root(g, core, T, topo, plan):
                 need(q, t_y)
                 queues[q].dma_start(T.y[h * 128:(h + 1) * 128, :], T.ysb[:, h * 128:(h + 1) * 128]).then_inc(
                     T.sem["yd%d" % h], 16)
+
+    stage_a(0)
+    for gi in range(len(groups)):
+        if gi + 1 <= last and (gi + 1) in AHEAD:
+            stage_a(gi + 1)
+        stage_b(gi)
+        if gi + 1 <= last and (gi + 1) not in AHEAD:
+            stage_a(gi + 1)
     for e in ("te", "ve", "se", "ge"):
         g.wait_ge(T.sem[e], cnt[e])
     g.wait_ge(T.sem.yd0, 16)

@@ -3,6 +3,7 @@ from concourse.mybir import AluOpType, AxisListType, ActivationFunctionType
 NR = 12
 NG = 4
 AHEAD = (1, 2)
+MID = (3,)
 
 SCRATCH = {
     "kd": ("dram", [128, 128], "bfloat16"),
@@ -156,8 +157,8 @@ def _root(g, core, T, topo, plan):
     Tb = [T.TA, T.TB]
     Ob = [T.O0, T.O1]
     last = len(groups) - 1
-    t_exp, t_cp, t_acc, t_a = {}, {}, {}, {}
-    negM, lacc, lblk, a = {}, {}, {}, {}
+    t_exp, t_cp, t_acc, t_a, t_sc, t_r = {}, {}, {}, {}, {}, {}
+    negM, lacc, lblk, a, rc = {}, {}, {}, {}, {}
     te.wait_ge(T.sem.lq, 16)
 
     def stage_a(gi):
@@ -200,13 +201,12 @@ def _root(g, core, T, topo, plan):
     def stage_b(gi):
         n = len(groups[gi])
         s0 = slot[groups[gi][0]][1]
-        rc, t_r, t_sc, t_PV = {}, {}, {}, {}
         if gi > 0:
             for h in (0, 1):
                 need("se", t_a[(gi, h)])
                 need("se", t_acc[(gi - 1, h)])
-                t_sc[h] = post(se.activation(T.acc[:, h * 128:(h + 1) * 128], T.acc[:, h * 128:(h + 1) * 128], Copy,
-                                             scale=a[(gi, h)]), "se")
+                t_sc[(gi, h)] = post(se.activation(T.acc[:, h * 128:(h + 1) * 128], T.acc[:, h * 128:(h + 1) * 128],
+                                                   Copy, scale=a[(gi, h)]), "se")
         for h in (0, 1):
             b0 = (h * NR + s0) * 128
             need("te", t_id)
@@ -236,6 +236,11 @@ def _root(g, core, T, topo, plan):
                 need("ve", t_l)
                 rc[h] = cols()
                 t_r[h] = post(ve.reciprocal(rc[h], lacc[(gi, h)]), "ve")
+
+    def stage_c(gi):
+        n = len(groups[gi])
+        s0 = slot[groups[gi][0]][1]
+        t_PV = {}
         te.wait_ge(T.sem["av%d" % gi], arrive(gi))
         for h in (0, 1):
             need("te", t_cp[(gi, h)])
@@ -251,7 +256,7 @@ def _root(g, core, T, topo, plan):
             if gi == 0:
                 t_acc[(gi, h)] = post(ve.tensor_copy(A, Ob[h][:, 0:128]), "ve")
             else:
-                need("ve", t_sc[h])
+                need("ve", t_sc[(gi, h)])
                 t_acc[(gi, h)] = post(ve.tensor_tensor(A, Ob[h][:, 0:128], A, AluOpType.add), "ve")
             if gi == last:
                 need("ve", t_acc[(gi, h)])
@@ -264,11 +269,15 @@ def _root(g, core, T, topo, plan):
 
     stage_a(0)
     for gi in range(len(groups)):
-        if gi + 1 <= last and (gi + 1) in AHEAD:
-            stage_a(gi + 1)
+        nxt = gi + 1 if gi < last else None
+        if nxt in AHEAD:
+            stage_a(nxt)
         stage_b(gi)
-        if gi + 1 <= last and (gi + 1) not in AHEAD:
-            stage_a(gi + 1)
+        if nxt in MID:
+            stage_a(nxt)
+        stage_c(gi)
+        if nxt is not None and nxt not in AHEAD and nxt not in MID:
+            stage_a(nxt)
     for e in ("te", "ve", "se", "ge"):
         g.wait_ge(T.sem[e], cnt[e])
     g.wait_ge(T.sem.yd0, 16)

@@ -1,9 +1,7 @@
 from concourse.mybir import AluOpType, AxisListType, ActivationFunctionType
 
 NR = 12
-NG = 4
-AHEAD = (1, 2)
-MID = (3,)
+NG = 3
 
 SCRATCH = {
     "kd": ("dram", [128, 128], "bfloat16"),
@@ -15,21 +13,19 @@ SCRATCH = {
     "Vall": ("sbuf", [128, NR * 128], "bfloat16"),
     "ones": ("sbuf", [128, 128], "bfloat16"),
     "ident": ("sbuf", [128, 128], "bfloat16"),
-    "P": ("sbuf", [128, 2 * NR * 128], "bfloat16"),
-    "PT": ("sbuf", [128, 2 * NR * 128], "bfloat16"),
-    "st": ("sbuf", [128, 128], "float32"),
-    "acc": ("sbuf", [128, 256], "float32"),
-    "ysb": ("sbuf", [128, 256], "bfloat16"),
+    "P": ("sbuf", [128, NR * 128], "bfloat16"),
+    "PT": ("sbuf", [128, NR * 128], "bfloat16"),
+    "st": ("sbuf", [128, 64], "float32"),
+    "acc": ("sbuf", [128, 128], "float32"),
+    "ysb": ("sbuf", [128, 128], "bfloat16"),
+    "yland": ("sbuf", [128, 128], "bfloat16"),
     "S0": ("psum", [128, 512], "float32"),
     "S1": ("psum", [128, 512], "float32"),
-    "S2": ("psum", [128, 512], "float32"),
-    "S3": ("psum", [128, 512], "float32"),
     "TA": ("psum", [128, 1024], "bfloat16"),
     "TB": ("psum", [128, 1024], "bfloat16"),
     "O0": ("psum", [128, 512], "float32"),
-    "O1": ("psum", [128, 512], "float32"),
 }
-SEMAPHORES = (["ldk", "ldv", "rka", "rva", "sent", "lq", "yd0", "yd1", "te", "ve", "se", "ge"]
+SEMAPHORES = (["ldk", "ldv", "rka", "rva", "sent", "lq", "yar", "yd0", "yd1", "te", "ve", "se", "ge"]
               + ["ak%d" % i for i in range(NG)] + ["av%d" % i for i in range(NG)])
 
 
@@ -38,6 +34,7 @@ def _bits(m):
 
 
 def _lowest(m, n):
+    n = min(n, _bits(m))
     out, b = 0, 1
     while n > 0:
         if m & b:
@@ -51,9 +48,11 @@ def _plan(T, topo):
     cores = list(T.cores)
     root = cores[T.root]
     near = [r for r, c in enumerate(cores) if c != root and topo.chip(c) == topo.chip(root)]
+    near.sort(key=lambda r: 0 if topo.die(cores[r]) == topo.die(root) else 1)
+    hub = cores[near[0]]
     far = [r for r, c in enumerate(cores) if topo.chip(c) != topo.chip(root)]
-    direct = [r for r in far if topo.may_write(cores[r], root)]
-    passed = [r for r in far if not topo.may_write(cores[r], root)]
+    direct = [r for r in far if topo.may_write(cores[r], hub)]
+    passed = [r for r in far if not topo.may_write(cores[r], hub)]
     via = {}
     for r in passed:
         c = cores[r]
@@ -62,55 +61,62 @@ def _plan(T, topo):
         cand = same + [d for d in cand if d not in same]
         free = [d for d in cand if d not in via.values()]
         via[r] = (free or cand)[0]
-    groups = [[T.root], near, direct, passed]
+    groups = [[T.root] + near, direct, passed]
     slot = {}
     for gi, grp in enumerate(groups):
         for r in grp:
             slot[r] = (gi, len(slot))
-    return cores, root, groups, slot, via
-
-
-def _send(g, T, topo, src, dst, out_ap, in_ap, rsem, n_eng):
-    rid, pid, _ = topo.addr(dst)
-    m = topo.mask(src, dst)
-    m = _lowest(m, min(n_eng, _bits(m)))
-    g.remote_dma(out_ap=out_ap, in_ap=in_ap, remote_sem=rsem, local_sem=T.sem.sent, pid=pid, routing_id=rid,
-                 dma_engine_mask=m)
-    return _bits(m)
+    return cores, root, hub, groups, slot, via
 
 
 NE = 8
 
 
+def _n(topo, src, dst):
+    return _bits(_lowest(topo.mask(src, dst), NE))
+
+
+def _send(g, T, topo, src, dst, out_ap, in_ap, rsem):
+    rid, pid, _ = topo.addr(dst)
+    g.remote_dma(out_ap=out_ap, in_ap=in_ap, remote_sem=rsem, local_sem=T.sem.sent, pid=pid, routing_id=rid,
+                 dma_engine_mask=_lowest(topo.mask(src, dst), NE))
+    return _n(topo, src, dst)
+
+
 def _sender(g, core, T, topo, rank, plan):
-    cores, root, groups, slot, via = plan
+    cores, root, hub, groups, slot, via = plan
     g.sync.dma_start(T.kd[:, :], T.k[:, :]).then_inc(T.sem.ldk, 16)
     g.scalar.dma_start(T.vd[:, :], T.v[:, :]).then_inc(T.sem.ldv, 16)
     sent = 0
     if rank in via:
         dst = cores[via[rank]]
         g.wait_ge(T.sem.ldk, 16)
-        sent += _send(g, T, topo, core, dst, T.rk[:, :], T.kd[:, :], T.sem.rka, NE)
+        sent += _send(g, T, topo, core, dst, T.rk[:, :], T.kd[:, :], T.sem.rka)
         g.wait_ge(T.sem.ldv, 16)
-        sent += _send(g, T, topo, core, dst, T.rv[:, :], T.vd[:, :], T.sem.rva, NE)
+        sent += _send(g, T, topo, core, dst, T.rv[:, :], T.vd[:, :], T.sem.rva)
     else:
         gi, s = slot[rank]
+        dsts = [hub, root] if gi == 0 else [hub]
         g.wait_ge(T.sem.ldk, 16)
-        sent += _send(g, T, topo, core, root, T.Kall[:, s * 128:(s + 1) * 128], T.kd[:, :], T.sem["ak%d" % gi], NE)
+        for d in dsts:
+            sent += _send(g, T, topo, core, d, T.Kall[:, s * 128:(s + 1) * 128], T.kd[:, :], T.sem["ak%d" % gi])
         g.wait_ge(T.sem.ldv, 16)
-        sent += _send(g, T, topo, core, root, T.Vall[:, s * 128:(s + 1) * 128], T.vd[:, :], T.sem["av%d" % gi], NE)
+        for d in dsts:
+            sent += _send(g, T, topo, core, d, T.Vall[:, s * 128:(s + 1) * 128], T.vd[:, :], T.sem["av%d" % gi])
         for r in [r for r in via if via[r] == rank]:
             gi, s = slot[r]
-            n_in = _bits(_lowest(topo.mask(cores[r], core), NE))
-            g.wait_ge(T.sem.rka, n_in)
-            sent += _send(g, T, topo, core, root, T.Kall[:, s * 128:(s + 1) * 128], T.rk[:, :], T.sem["ak%d" % gi], NE)
-            g.wait_ge(T.sem.rva, n_in)
-            sent += _send(g, T, topo, core, root, T.Vall[:, s * 128:(s + 1) * 128], T.rv[:, :], T.sem["av%d" % gi], NE)
+            g.wait_ge(T.sem.rka, _n(topo, cores[r], core))
+            sent += _send(g, T, topo, core, hub, T.Kall[:, s * 128:(s + 1) * 128], T.rk[:, :], T.sem["ak%d" % gi])
+            g.wait_ge(T.sem.rva, _n(topo, cores[r], core))
+            sent += _send(g, T, topo, core, hub, T.Vall[:, s * 128:(s + 1) * 128], T.rv[:, :], T.sem["av%d" % gi])
     g.wait_ge(T.sem.sent, sent)
 
 
-def _root(g, core, T, topo, plan):
-    cores, root, groups, slot, via = plan
+def _worker(g, core, T, topo, rank, plan):
+    cores, root, hub, groups, slot, via = plan
+    is_root = core == root
+    other = hub if is_root else root
+    h = 0 if is_root else 1
     te, ve, se = g.tensor, g.vector, g.scalar
     Exp, Copy = ActivationFunctionType.Exp, ActivationFunctionType.Copy
     cnt = {"te": 0, "ve": 0, "se": 0, "ge": 0}
@@ -138,150 +144,151 @@ def _root(g, core, T, topo, plan):
         ncol[0] += n
         return T.st[:, c:c + n]
 
-    g.sync.dma_start(T.qs[:, :], T.q[:, :]).then_inc(T.sem.lq, 16)
-    g.scalar.dma_start(T.Kall[:, 0:128], T.k[:, :]).then_inc(T.sem.ak0, 16)
-    g.sync.dma_start(T.Vall[:, 0:128], T.v[:, :]).then_inc(T.sem.av0, 16)
-    need("ge", post(ve.memset(T.ones[:, :], 1.0), "ve"))
+    def span(gi):
+        s0 = slot[groups[gi][0]][1]
+        return s0 * 128, (s0 + len(groups[gi])) * 128
+
+    ms = slot[rank][1]
+    mine = (ms * 128, (ms + 1) * 128)
+    if is_root:
+        g.sync.dma_start(T.qs[:, :], T.q[:, :]).then_inc(T.sem.lq, 16)
+    g.scalar.dma_start(T.Kall[:, mine[0]:mine[1]], T.k[:, :]).then_inc(T.sem.ldk, 16)
+    g.sync.dma_start(T.Vall[:, mine[0]:mine[1]], T.v[:, :]).then_inc(T.sem.ldv, 16)
+    t_ones = post(ve.memset(T.ones[:, :], 1.0), "ve")
+    sent = 0
+    if is_root:
+        g.wait_ge(T.sem.lq, 16)
+        sent += _send(g, T, topo, core, other, T.qs[:, :], T.qs[:, :], T.sem.lq)
+    g.wait_ge(T.sem.ldk, 16)
+    sent += _send(g, T, topo, core, other, T.Kall[:, mine[0]:mine[1]], T.Kall[:, mine[0]:mine[1]], T.sem.ak0)
+    g.wait_ge(T.sem.ldv, 16)
+    sent += _send(g, T, topo, core, other, T.Vall[:, mine[0]:mine[1]], T.Vall[:, mine[0]:mine[1]], T.sem.av0)
+    need("ge", t_ones)
     t_id = post(g.affine_select(T.ident[:, :], T.ones[:, :], [[-1, 128]], AluOpType.is_equal, 0.0, 0, 1), "ge")
 
     def arrive(gi):
         if gi == 0:
-            return 16
-        tot = 0
-        for r in groups[gi]:
-            src = cores[via[r]] if r in via else cores[r]
-            tot += _bits(_lowest(topo.mask(src, root), NE))
-        return tot
+            return sum(_n(topo, cores[r], core) for r in groups[0] if cores[r] != core)
+        if is_root:
+            return _n(topo, hub, root)
+        return sum(_n(topo, cores[via[r]] if r in via else cores[r], core) for r in groups[gi])
 
-    Sb = [T.S0, T.S1, T.S2, T.S3]
+    if not is_root:
+        for gi in range(1, len(groups)):
+            c0, c1 = span(gi)
+            g.wait_ge(T.sem["ak%d" % gi], arrive(gi))
+            sent += _send(g, T, topo, core, root, T.Kall[:, c0:c1], T.Kall[:, c0:c1], T.sem["ak%d" % gi])
+            g.wait_ge(T.sem["av%d" % gi], arrive(gi))
+            sent += _send(g, T, topo, core, root, T.Vall[:, c0:c1], T.Vall[:, c0:c1], T.sem["av%d" % gi])
+
+    Sb = [T.S0, T.S1]
     Tb = [T.TA, T.TB]
-    Ob = [T.O0, T.O1]
     last = len(groups) - 1
     t_exp, t_cp, t_acc, t_a, t_sc, t_r = {}, {}, {}, {}, {}, {}
     negM, lacc, lblk, a, rc = {}, {}, {}, {}, {}
-    te.wait_ge(T.sem.lq, 16)
+    te.wait_ge(T.sem.lq, 16 if is_root else _n(topo, root, core))
+    te.wait_ge(T.sem.ldk, 16)
 
     def stage_a(gi):
         n = len(groups[gi])
-        s0 = slot[groups[gi][0]][1]
+        c0, c1 = span(gi)
+        S = Sb[gi % 2]
         te.wait_ge(T.sem["ak%d" % gi], arrive(gi))
-        t_S, t_M = {}, {}
-        for h in (0, 1):
-            if gi >= 2:
-                need("te", t_exp[(gi - 2, h, len(groups[gi - 2]) - 1)])
-            t_S[h] = post(te.matmul(Sb[(gi % 2) * 2 + h][:, 0:128 * n], T.qs[:, h * 128:(h + 1) * 128],
-                                    T.Kall[:, s0 * 128:(s0 + n) * 128], True, True), "te")
-        for h in (0, 1):
-            need("ve", t_S[h])
-            nm = cols()
-            t = post(ve.tensor_reduce(nm, Sb[(gi % 2) * 2 + h][:, 0:128 * n], AxisListType.X, AluOpType.max,
-                                      negate=True), "ve")
-            if gi > 0:
-                need("ve", t)
-                nM = cols()
-                t = post(ve.tensor_tensor(nM, negM[(gi - 1, h)], nm, AluOpType.min), "ve")
-                nm = nM
-            negM[(gi, h)] = nm
-            t_M[h] = t
-        for h in (0, 1):
-            need("se", t_M[h])
-            lblk[(gi, h)] = cols(n)
-            for i in range(n):
-                b = (h * NR + s0 + i) * 128
-                t_exp[(gi, h, i)] = post(se.activation(T.P[:, b:b + 128],
-                                                       Sb[(gi % 2) * 2 + h][:, i * 128:(i + 1) * 128],
-                                                       Exp, bias=negM[(gi, h)], scale=1.0,
-                                                       accum_out=lblk[(gi, h)][:, i:i + 1]), "se")
+        if gi >= 2:
+            need("te", t_exp[(gi - 2, len(groups[gi - 2]) - 1)])
+        t = post(te.matmul(S[:, 0:128 * n], T.qs[:, h * 128:(h + 1) * 128], T.Kall[:, c0:c1], True, True), "te")
+        need("ve", t)
+        nm = cols()
+        t = post(ve.tensor_reduce(nm, S[:, 0:128 * n], AxisListType.X, AluOpType.max, negate=True), "ve")
         if gi > 0:
-            for h in (0, 1):
-                a[(gi, h)] = cols()
-                t_a[(gi, h)] = post(se.activation(a[(gi, h)], negM[(gi - 1, h)], Exp, bias=negM[(gi, h)],
-                                                  scale=-1.0), "se")
+            need("ve", t)
+            nM = cols()
+            t = post(ve.tensor_tensor(nM, negM[gi - 1], nm, AluOpType.min), "ve")
+            nm = nM
+        negM[gi] = nm
+        need("se", t)
+        lblk[gi] = cols(n)
+        for i in range(n):
+            t_exp[(gi, i)] = post(se.activation(T.P[:, c0 + i * 128:c0 + (i + 1) * 128], S[:, i * 128:(i + 1) * 128],
+                                                Exp, bias=negM[gi], scale=1.0, accum_out=lblk[gi][:, i:i + 1]), "se")
+        if gi > 0:
+            a[gi] = cols()
+            t_a[gi] = post(se.activation(a[gi], negM[gi - 1], Exp, bias=negM[gi], scale=-1.0), "se")
 
     def stage_b(gi):
         n = len(groups[gi])
-        s0 = slot[groups[gi][0]][1]
+        c0, c1 = span(gi)
         if gi > 0:
-            for h in (0, 1):
-                need("se", t_a[(gi, h)])
-                need("se", t_acc[(gi - 1, h)])
-                t_sc[(gi, h)] = post(se.activation(T.acc[:, h * 128:(h + 1) * 128], T.acc[:, h * 128:(h + 1) * 128],
-                                                   Copy, scale=a[(gi, h)]), "se")
-        for h in (0, 1):
-            b0 = (h * NR + s0) * 128
-            need("te", t_id)
-            need("te", t_cp.get((gi - 1, h)))
-            for i in range(n):
-                need("te", t_exp[(gi, h, i)])
-                t = post(te.transpose(Tb[h][:, i * 128:(i + 1) * 128], T.P[:, b0 + i * 128:b0 + (i + 1) * 128],
-                                      T.ident[:, :]), "te")
+            need("se", t_a[gi])
+            need("se", t_acc[gi - 1])
+            t_sc[gi] = post(se.activation(T.acc[:, :], T.acc[:, :], Copy, scale=a[gi]), "se")
+        need("te", t_id)
+        for half in (0, 1):
+            lo, hi = half * (n // 2), (n // 2 if half == 0 else n)
+            need("te", t_cp.get((gi - 1, half)))
+            for i in range(lo, hi):
+                need("te", t_exp[(gi, i)])
+                t = post(te.transpose(Tb[half][:, (i - lo) * 128:(i - lo + 1) * 128],
+                                      T.P[:, c0 + i * 128:c0 + (i + 1) * 128], T.ident[:, :]), "te")
             need("ve", t)
-            t_cp[(gi, h)] = post(ve.tensor_copy(T.PT[:, b0:b0 + n * 128], Tb[h][:, 0:n * 128]), "ve")
-            need("ve", t_exp[(gi, h, n - 1)])
-            if n > 1:
-                ls = cols()
-                t_l = post(ve.tensor_reduce(ls, lblk[(gi, h)], AxisListType.X, AluOpType.add), "ve")
-            else:
-                ls = lblk[(gi, h)]
-                t_l = None
-            if gi == 0:
-                lacc[(gi, h)] = ls
-            else:
-                need("ve", t_a[(gi, h)])
-                need("ve", t_l)
-                lacc[(gi, h)] = cols()
-                t_l = post(ve.tensor_scalar(lacc[(gi, h)], lacc[(gi - 1, h)], a[(gi, h)], ls, AluOpType.mult,
-                                            AluOpType.add), "ve")
-            if gi == last:
-                need("ve", t_l)
-                rc[h] = cols()
-                t_r[h] = post(ve.reciprocal(rc[h], lacc[(gi, h)]), "ve")
+            t_cp[(gi, half)] = post(ve.tensor_copy(T.PT[:, c0 + lo * 128:c0 + hi * 128],
+                                                   Tb[half][:, 0:(hi - lo) * 128]), "ve")
+        need("ve", t_exp[(gi, n - 1)])
+        ls = cols()
+        t_l = post(ve.tensor_reduce(ls, lblk[gi], AxisListType.X, AluOpType.add), "ve")
+        if gi == 0:
+            lacc[gi] = ls
+        else:
+            need("ve", t_a[gi])
+            need("ve", t_l)
+            lacc[gi] = cols()
+            t_l = post(ve.tensor_scalar(lacc[gi], lacc[gi - 1], a[gi], ls, AluOpType.mult, AluOpType.add), "ve")
+        if gi == last:
+            need("ve", t_l)
+            rc[0] = cols()
+            t_r[0] = post(ve.reciprocal(rc[0], lacc[gi]), "ve")
 
     def stage_c(gi):
         n = len(groups[gi])
-        s0 = slot[groups[gi][0]][1]
-        t_PV = {}
+        c0, c1 = span(gi)
+        if gi == 0:
+            te.wait_ge(T.sem.ldv, 16)
         te.wait_ge(T.sem["av%d" % gi], arrive(gi))
-        for h in (0, 1):
-            need("te", t_cp[(gi, h)])
-            need("te", t_acc.get((gi - 1, h)))
-            for i in range(n):
-                b = (h * NR + s0 + i) * 128
-                ins = te.matmul(Ob[h][:, 0:128], T.PT[:, b:b + 128], T.Vall[:, (s0 + i) * 128:(s0 + i + 1) * 128],
-                                i == 0, i == n - 1)
-            t_PV[h] = post(ins, "te")
-        for h in (0, 1):
-            A = T.acc[:, h * 128:(h + 1) * 128]
-            need("ve", t_PV[h])
-            if gi == 0:
-                t_acc[(gi, h)] = post(ve.tensor_copy(A, Ob[h][:, 0:128]), "ve")
-            else:
-                need("ve", t_sc[(gi, h)])
-                t_acc[(gi, h)] = post(ve.tensor_tensor(A, Ob[h][:, 0:128], A, AluOpType.add), "ve")
-            if gi == last:
-                need("ve", t_acc[(gi, h)])
-                need("ve", t_r[h])
-                t_y = post(ve.tensor_scalar(T.ysb[:, h * 128:(h + 1) * 128], A, rc[h], None, AluOpType.mult), "ve")
-                q = "sy" if h == 0 else "se"
-                need(q, t_y)
-                queues[q].dma_start(T.y[h * 128:(h + 1) * 128, :], T.ysb[:, h * 128:(h + 1) * 128]).then_inc(
-                    T.sem["yd%d" % h], 16)
+        need("te", t_cp[(gi, 1)])
+        need("te", t_acc.get(gi - 1))
+        for i in range(n):
+            ins = te.matmul(T.O0[:, 0:128], T.PT[:, c0 + i * 128:c0 + (i + 1) * 128],
+                            T.Vall[:, c0 + i * 128:c0 + (i + 1) * 128], i == 0, i == n - 1)
+        need("ve", post(ins, "te"))
+        if gi == 0:
+            t_acc[gi] = post(ve.tensor_copy(T.acc[:, :], T.O0[:, 0:128]), "ve")
+        else:
+            need("ve", t_sc[gi])
+            t_acc[gi] = post(ve.tensor_tensor(T.acc[:, :], T.O0[:, 0:128], T.acc[:, :], AluOpType.add), "ve")
 
     stage_a(0)
     for gi in range(len(groups)):
-        nxt = gi + 1 if gi < last else None
-        if nxt in AHEAD:
-            stage_a(nxt)
+        if gi < last:
+            stage_a(gi + 1)
         stage_b(gi)
-        if nxt in MID:
-            stage_a(nxt)
         stage_c(gi)
-        if nxt is not None and nxt not in AHEAD and nxt not in MID:
-            stage_a(nxt)
+    need("ve", t_acc[last])
+    need("ve", t_r[0])
+    t_y = post(ve.tensor_scalar(T.ysb[:, :], T.acc[:, :], rc[0], None, AluOpType.mult), "ve")
+    if is_root:
+        need("sy", t_y)
+        g.sync.dma_start(T.y[0:128, :], T.ysb[:, :]).then_inc(T.sem.yd0, 16)
+        se.wait_ge(T.sem.yar, _n(topo, hub, root))
+        se.dma_start(T.y[128:256, :], T.yland[:, :]).then_inc(T.sem.yd1, 16)
+    else:
+        need("ge", t_y)
+        sent += _send(g, T, topo, core, root, T.yland[:, :], T.ysb[:, :], T.sem.yar)
     for e in ("te", "ve", "se", "ge"):
         g.wait_ge(T.sem[e], cnt[e])
-    g.wait_ge(T.sem.yd0, 16)
-    g.wait_ge(T.sem.yd1, 16)
+    g.wait_ge(T.sem.sent, sent)
+    if is_root:
+        g.wait_ge(T.sem.yd0, 16)
+        g.wait_ge(T.sem.yd1, 16)
 
 
 def rank_program(g, core, T, topo):
@@ -289,7 +296,7 @@ def rank_program(g, core, T, topo):
     if rank is None:
         return
     plan = _plan(T, topo)
-    if rank == T.root:
-        _root(g, core, T, topo, plan)
+    if core == plan[1] or core == plan[2]:
+        _worker(g, core, T, topo, rank, plan)
     else:
         _sender(g, core, T, topo, rank, plan)

@@ -11,6 +11,7 @@ SCRATCH = {
     "qs": ("sbuf", [128, 256], "bfloat16"),
     "Kall": ("sbuf", [128, NR * 128], "bfloat16"),
     "Vall": ("sbuf", [128, NR * 128], "bfloat16"),
+    "zer": ("sbuf", [128, 128], "bfloat16"),
     "ones": ("sbuf", [128, 128], "bfloat16"),
     "ident": ("sbuf", [128, 128], "bfloat16"),
     "P": ("sbuf", [128, NR * 128], "bfloat16"),
@@ -19,8 +20,10 @@ SCRATCH = {
     "acc": ("sbuf", [128, 128], "float32"),
     "ysb": ("sbuf", [128, 128], "bfloat16"),
     "yland": ("sbuf", [128, 128], "bfloat16"),
-    "S0": ("psum", [128, 512], "float32"),
-    "S1": ("psum", [128, 512], "float32"),
+    "S0a": ("psum", [128, 512], "float32"),
+    "S0b": ("psum", [128, 512], "float32"),
+    "S1a": ("psum", [128, 512], "float32"),
+    "S1b": ("psum", [128, 512], "float32"),
     "TA": ("psum", [128, 1024], "bfloat16"),
     "TB": ("psum", [128, 1024], "bfloat16"),
     "O0": ("psum", [128, 512], "float32"),
@@ -154,11 +157,12 @@ def _worker(g, core, T, topo, rank, plan):
         g.sync.dma_start(T.qs[:, :], T.q[:, :]).then_inc(T.sem.lq, 16)
     g.scalar.dma_start(T.Kall[:, mine[0]:mine[1]], T.k[:, :]).then_inc(T.sem.ldk, 16)
     g.sync.dma_start(T.Vall[:, mine[0]:mine[1]], T.v[:, :]).then_inc(T.sem.ldv, 16)
-    t_ones = post(ve.memset(T.ones[:, :], 1.0), "ve")
+    need("se", post(ve.memset(T.zer[:, :], 0.0), "ve"))
+    t_ones = post(se.activation(T.ones[:, :], T.zer[:, :], Exp), "se")
     sent = 0
     if is_root:
         g.wait_ge(T.sem.lq, 16)
-        sent += _send(g, T, topo, core, other, T.qs[:, :], T.qs[:, :], T.sem.lq)
+        sent += _send(g, T, topo, core, other, T.qs[:, 128:256], T.qs[:, 128:256], T.sem.lq)
     g.wait_ge(T.sem.ldk, 16)
     sent += _send(g, T, topo, core, other, T.Kall[:, mine[0]:mine[1]], T.Kall[:, mine[0]:mine[1]], T.sem.ak0)
     g.wait_ge(T.sem.ldv, 16)
@@ -181,7 +185,8 @@ def _worker(g, core, T, topo, rank, plan):
             g.wait_ge(T.sem["av%d" % gi], arrive(gi))
             sent += _send(g, T, topo, core, root, T.Vall[:, c0:c1], T.Vall[:, c0:c1], T.sem["av%d" % gi])
 
-    Sb = [T.S0, T.S1]
+    Sb = [[T.S0a, T.S0b], [T.S1a, T.S1b]]
+    mcol = cols(3 * len(groups) + 1)
     Tb = [T.TA, T.TB]
     last = len(groups) - 1
     t_exp, t_cp, t_acc, t_a, t_sc, t_r = {}, {}, {}, {}, {}, {}
@@ -193,23 +198,28 @@ def _worker(g, core, T, topo, rank, plan):
         n = len(groups[gi])
         c0, c1 = span(gi)
         S = Sb[gi % 2]
+        hn = n // 2
         te.wait_ge(T.sem["ak%d" % gi], arrive(gi))
         if gi >= 2:
             need("te", t_exp[(gi - 2, len(groups[gi - 2]) - 1)])
-        t = post(te.matmul(S[:, 0:128 * n], T.qs[:, h * 128:(h + 1) * 128], T.Kall[:, c0:c1], True, True), "te")
+        tm = []
+        for half, (lo, hi) in enumerate(((0, hn), (hn, n))):
+            tm.append(post(te.matmul(S[half][:, 0:128 * (hi - lo)], T.qs[:, h * 128:(h + 1) * 128],
+                                     T.Kall[:, c0 + lo * 128:c0 + hi * 128], True, True), "te"))
+        for half, (lo, hi) in enumerate(((0, hn), (hn, n))):
+            need("ve", tm[half])
+            t = post(ve.tensor_reduce(mcol[:, 3 * gi + 1 + half:3 * gi + 2 + half], S[half][:, 0:128 * (hi - lo)],
+                                      AxisListType.X, AluOpType.max, negate=True), "ve")
         need("ve", t)
-        nm = cols()
-        t = post(ve.tensor_reduce(nm, S[:, 0:128 * n], AxisListType.X, AluOpType.max, negate=True), "ve")
-        if gi > 0:
-            need("ve", t)
-            nM = cols()
-            t = post(ve.tensor_tensor(nM, negM[gi - 1], nm, AluOpType.min), "ve")
-            nm = nM
+        nm = mcol[:, 3 * gi + 3:3 * gi + 4]
+        t = post(ve.tensor_reduce(nm, mcol[:, (3 * gi if gi > 0 else 1):3 * gi + 3], AxisListType.X, AluOpType.min),
+                 "ve")
         negM[gi] = nm
         need("se", t)
         lblk[gi] = cols(n)
         for i in range(n):
-            t_exp[(gi, i)] = post(se.activation(T.P[:, c0 + i * 128:c0 + (i + 1) * 128], S[:, i * 128:(i + 1) * 128],
+            t_exp[(gi, i)] = post(se.activation(T.P[:, c0 + i * 128:c0 + (i + 1) * 128],
+                                                S[i // hn][:, (i % hn) * 128:(i % hn + 1) * 128],
                                                 Exp, bias=negM[gi], scale=1.0, accum_out=lblk[gi][:, i:i + 1]), "se")
         if gi > 0:
             a[gi] = cols()
@@ -254,9 +264,9 @@ def _worker(g, core, T, topo, rank, plan):
         if gi == 0:
             te.wait_ge(T.sem.ldv, 16)
         te.wait_ge(T.sem["av%d" % gi], arrive(gi))
-        need("te", t_cp[(gi, 1)])
         need("te", t_acc.get(gi - 1))
         for i in range(n):
+            need("te", t_cp[(gi, 0 if i < n // 2 else 1)])
             ins = te.matmul(T.O0[:, 0:128], T.PT[:, c0 + i * 128:c0 + (i + 1) * 128],
                             T.Vall[:, c0 + i * 128:c0 + (i + 1) * 128], i == 0, i == n - 1)
         need("ve", post(ins, "te"))

@@ -1,7 +1,7 @@
+from concourse.bass import DstId, RemoteDMATransfer
 from concourse.mybir import AluOpType, AxisListType, ActivationFunctionType
 
-NR = 12
-NG = 3
+VS = 136
 
 SCRATCH = {
     "kd": ("dram", [128, 128], "bfloat16"),
@@ -9,17 +9,22 @@ SCRATCH = {
     "rk": ("dram", [128, 128], "bfloat16"),
     "rv": ("dram", [128, 128], "bfloat16"),
     "qs": ("sbuf", [128, 256], "bfloat16"),
-    "Kall": ("sbuf", [128, NR * 128], "bfloat16"),
-    "Vall": ("sbuf", [128, NR * 128], "bfloat16"),
+    "ks": ("sbuf", [128, 128], "bfloat16"),
+    "vs": ("sbuf", [128, 128], "bfloat16"),
+    "Kall": ("sbuf", [128, 4 * 128], "bfloat16"),
+    "Vall": ("sbuf", [128, 4 * VS], "bfloat16"),
     "zer": ("sbuf", [128, 128], "bfloat16"),
     "ones": ("sbuf", [128, 128], "bfloat16"),
     "ident": ("sbuf", [128, 128], "bfloat16"),
-    "P": ("sbuf", [128, NR * 128], "bfloat16"),
-    "PT": ("sbuf", [128, NR * 128], "bfloat16"),
-    "st": ("sbuf", [128, 64], "float32"),
-    "acc": ("sbuf", [128, 128], "float32"),
-    "ysb": ("sbuf", [128, 128], "bfloat16"),
-    "yland": ("sbuf", [128, 128], "bfloat16"),
+    "P": ("sbuf", [128, 8 * 128], "bfloat16"),
+    "PT": ("sbuf", [128, 8 * 128], "bfloat16"),
+    "st": ("sbuf", [128, 32], "float32"),
+    "pk": ("sbuf", [128, 2 * VS], "bfloat16"),
+    "pkl": ("sbuf", [128, 4 * VS], "bfloat16"),
+    "ml0": ("sbuf", [128, 2], "float32"),
+    "ml1": ("sbuf", [128, 2], "float32"),
+    "dg": ("sbuf", [128, 4 * 128], "bfloat16"),
+    "ysb": ("sbuf", [128, 256], "bfloat16"),
     "S0a": ("psum", [128, 512], "float32"),
     "S0b": ("psum", [128, 512], "float32"),
     "S1a": ("psum", [128, 512], "float32"),
@@ -27,9 +32,10 @@ SCRATCH = {
     "TA": ("psum", [128, 1024], "bfloat16"),
     "TB": ("psum", [128, 1024], "bfloat16"),
     "O0": ("psum", [128, 512], "float32"),
+    "O1": ("psum", [128, 512], "float32"),
 }
-SEMAPHORES = (["ldk", "ldv", "rka", "rva", "sent", "lq", "yar", "yd0", "yd1", "te", "ve", "se", "ge"]
-              + ["ak%d" % i for i in range(NG)] + ["av%d" % i for i in range(NG)])
+SEMAPHORES = ["ldk", "ldv", "rka", "rva", "sent", "lq", "yd0", "yd1", "te", "ve", "se", "ge", "ak0", "ak1", "av",
+              "am0", "am1", "ap0", "ap1"]
 
 
 def _bits(m):
@@ -52,10 +58,9 @@ def _plan(T, topo):
     root = cores[T.root]
     near = [r for r, c in enumerate(cores) if c != root and topo.chip(c) == topo.chip(root)]
     near.sort(key=lambda r: 0 if topo.die(cores[r]) == topo.die(root) else 1)
-    hub = cores[near[0]]
     far = [r for r, c in enumerate(cores) if topo.chip(c) != topo.chip(root)]
-    direct = [r for r in far if topo.may_write(cores[r], hub)]
-    passed = [r for r in far if not topo.may_write(cores[r], hub)]
+    direct = [r for r in far if topo.may_write(cores[r], root)]
+    passed = [r for r in far if not topo.may_write(cores[r], root)]
     via = {}
     for r in passed:
         c = cores[r]
@@ -64,12 +69,13 @@ def _plan(T, topo):
         cand = same + [d for d in cand if d not in same]
         free = [d for d in cand if d not in via.values()]
         via[r] = (free or cand)[0]
-    groups = [[T.root] + near, direct, passed]
-    slot = {}
-    for gi, grp in enumerate(groups):
-        for r in grp:
-            slot[r] = (gi, len(slot))
-    return cores, root, hub, groups, slot, via
+    groups = [[near[1], near[2], T.root, direct[0]], [near[0]] + direct[1:], passed]
+    W = [cores[near[0]], cores[near[1]], root]
+    place = {}
+    for w, grp in enumerate(groups):
+        for s, r in enumerate(grp):
+            place[r] = (W[w], s)
+    return cores, root, W, groups, place, via
 
 
 NE = 8
@@ -86,8 +92,20 @@ def _send(g, T, topo, src, dst, out_ap, in_ap, rsem):
     return _n(topo, src, dst)
 
 
+def _kslot(T, s):
+    return T.Kall[:, s * 128:(s + 1) * 128]
+
+
+def _vslot(T, s):
+    return T.Vall[:, s * VS:s * VS + 128]
+
+
+def _ksem(T, s):
+    return T.sem["ak%d" % (s // 2)]
+
+
 def _sender(g, core, T, topo, rank, plan):
-    cores, root, hub, groups, slot, via = plan
+    cores, root, W, groups, place, via = plan
     g.sync.dma_start(T.kd[:, :], T.k[:, :]).then_inc(T.sem.ldk, 16)
     g.scalar.dma_start(T.vd[:, :], T.v[:, :]).then_inc(T.sem.ldv, 16)
     sent = 0
@@ -98,30 +116,29 @@ def _sender(g, core, T, topo, rank, plan):
         g.wait_ge(T.sem.ldv, 16)
         sent += _send(g, T, topo, core, dst, T.rv[:, :], T.vd[:, :], T.sem.rva)
     else:
-        gi, s = slot[rank]
-        dsts = [hub, root] if gi == 0 else [hub]
+        dst, s = place[rank]
         g.wait_ge(T.sem.ldk, 16)
-        for d in dsts:
-            sent += _send(g, T, topo, core, d, T.Kall[:, s * 128:(s + 1) * 128], T.kd[:, :], T.sem["ak%d" % gi])
+        sent += _send(g, T, topo, core, dst, _kslot(T, s), T.kd[:, :], _ksem(T, s))
         g.wait_ge(T.sem.ldv, 16)
-        for d in dsts:
-            sent += _send(g, T, topo, core, d, T.Vall[:, s * 128:(s + 1) * 128], T.vd[:, :], T.sem["av%d" % gi])
+        sent += _send(g, T, topo, core, dst, _vslot(T, s), T.vd[:, :], T.sem.av)
         for r in [r for r in via if via[r] == rank]:
-            gi, s = slot[r]
+            dst, s = place[r]
             g.wait_ge(T.sem.rka, _n(topo, cores[r], core))
-            sent += _send(g, T, topo, core, hub, T.Kall[:, s * 128:(s + 1) * 128], T.rk[:, :], T.sem["ak%d" % gi])
+            sent += _send(g, T, topo, core, dst, _kslot(T, s), T.rk[:, :], _ksem(T, s))
             g.wait_ge(T.sem.rva, _n(topo, cores[r], core))
-            sent += _send(g, T, topo, core, hub, T.Vall[:, s * 128:(s + 1) * 128], T.rv[:, :], T.sem["av%d" % gi])
+            sent += _send(g, T, topo, core, dst, _vslot(T, s), T.rv[:, :], T.sem.av)
     g.wait_ge(T.sem.sent, sent)
 
 
 def _worker(g, core, T, topo, rank, plan):
-    cores, root, hub, groups, slot, via = plan
+    cores, root, W, groups, place, via = plan
     is_root = core == root
-    other = hub if is_root else root
-    h = 0 if is_root else 1
+    w = W.index(core)
+    grp = groups[w]
+    n = len(grp)
+    hn = n // 2
     te, ve, se = g.tensor, g.vector, g.scalar
-    Exp, Copy = ActivationFunctionType.Exp, ActivationFunctionType.Copy
+    Exp = ActivationFunctionType.Exp
     cnt = {"te": 0, "ve": 0, "se": 0, "ge": 0}
     seen = {}
     queues = {"te": te, "ve": ve, "se": se, "ge": g, "sy": g.sync}
@@ -134,165 +151,158 @@ def _worker(g, core, T, topo, rank, plan):
     def need(q, tok):
         if tok is None:
             return
-        e, n = tok
-        if seen.get((q, e), 0) >= n:
+        e, m = tok
+        if seen.get((q, e), 0) >= m:
             return
-        seen[(q, e)] = n
-        queues[q].wait_ge(T.sem[e], n)
+        seen[(q, e)] = m
+        queues[q].wait_ge(T.sem[e], m)
 
     ncol = [0]
 
-    def cols(n=1):
+    def cols(m=1):
         c = ncol[0]
-        ncol[0] += n
-        return T.st[:, c:c + n]
+        ncol[0] += m
+        return T.st[:, c:c + m]
 
-    def span(gi):
-        s0 = slot[groups[gi][0]][1]
-        return s0 * 128, (s0 + len(groups[gi])) * 128
-
-    ms = slot[rank][1]
-    mine = (ms * 128, (ms + 1) * 128)
     if is_root:
         g.sync.dma_start(T.qs[:, :], T.q[:, :]).then_inc(T.sem.lq, 16)
-    g.scalar.dma_start(T.Kall[:, mine[0]:mine[1]], T.k[:, :]).then_inc(T.sem.ldk, 16)
-    g.sync.dma_start(T.Vall[:, mine[0]:mine[1]], T.v[:, :]).then_inc(T.sem.ldv, 16)
+    g.scalar.dma_start(T.ks[:, :], T.k[:, :]).then_inc(T.sem.ldk, 16)
+    g.sync.dma_start(T.vs[:, :], T.v[:, :]).then_inc(T.sem.ldv, 16)
     need("se", post(ve.memset(T.zer[:, :], 0.0), "ve"))
     t_ones = post(se.activation(T.ones[:, :], T.zer[:, :], Exp), "se")
+    for s in range(n):
+        t_vo = post(ve.memset(T.Vall[:, s * VS + 128:(s + 1) * VS], 1.0), "ve")
     sent = 0
     if is_root:
         g.wait_ge(T.sem.lq, 16)
-        sent += _send(g, T, topo, core, other, T.qs[:, 128:256], T.qs[:, 128:256], T.sem.lq)
+        trs, used = [], 0
+        for d in W[:2]:
+            rid, pid, _ = topo.addr(d)
+            m = _lowest(topo.mask(core, d) & ~used, NE)
+            used |= m
+            trs.append(RemoteDMATransfer(dst_ids=[DstId(rid=rid, pnc=pid)], dma_engine_mask=m, remote_sem=T.sem.lq,
+                                         src=T.qs[:, :], dst=T.qs[:, :]))
+            sent += _bits(m)
+        g.remote_dma_fused(trs, local_sem=T.sem.sent)
+    dst, s = place[rank]
     g.wait_ge(T.sem.ldk, 16)
-    sent += _send(g, T, topo, core, other, T.Kall[:, mine[0]:mine[1]], T.Kall[:, mine[0]:mine[1]], T.sem.ak0)
+    sent += _send(g, T, topo, core, dst, _kslot(T, s), T.ks[:, :], _ksem(T, s))
     g.wait_ge(T.sem.ldv, 16)
-    sent += _send(g, T, topo, core, other, T.Vall[:, mine[0]:mine[1]], T.Vall[:, mine[0]:mine[1]], T.sem.av0)
+    sent += _send(g, T, topo, core, dst, _vslot(T, s), T.vs[:, :], T.sem.av)
     need("ge", t_ones)
     t_id = post(g.affine_select(T.ident[:, :], T.ones[:, :], [[-1, 128]], AluOpType.is_equal, 0.0, 0, 1), "ge")
 
-    def arrive(gi):
-        if gi == 0:
-            return sum(_n(topo, cores[r], core) for r in groups[0] if cores[r] != core)
-        if is_root:
-            return _n(topo, hub, root)
-        return sum(_n(topo, cores[via[r]] if r in via else cores[r], core) for r in groups[gi])
+    def arrive(rs):
+        return sum(_n(topo, cores[via[r]] if r in via else cores[r], core) for r in rs)
 
-    if not is_root:
-        for gi in range(1, len(groups)):
-            c0, c1 = span(gi)
-            g.wait_ge(T.sem["ak%d" % gi], arrive(gi))
-            sent += _send(g, T, topo, core, root, T.Kall[:, c0:c1], T.Kall[:, c0:c1], T.sem["ak%d" % gi])
-            g.wait_ge(T.sem["av%d" % gi], arrive(gi))
-            sent += _send(g, T, topo, core, root, T.Vall[:, c0:c1], T.Vall[:, c0:c1], T.sem["av%d" % gi])
-
+    n_pk = sum(_n(topo, d, root) for d in W[:2])
     Sb = [[T.S0a, T.S0b], [T.S1a, T.S1b]]
-    mcol = cols(3 * len(groups) + 1)
     Tb = [T.TA, T.TB]
-    last = len(groups) - 1
-    t_exp, t_cp, t_acc, t_a, t_sc, t_r = {}, {}, {}, {}, {}, {}
-    negM, lacc, lblk, a, rc = {}, {}, {}, {}, {}
+    Ob = [T.O0, T.O1]
+    ml = [T.ml0, T.ml1]
+    t_exp, t_cp, t_M, t_b, t_dg, t_o = {}, {}, {}, {}, {}, {}
+    negM, bc = {}, {}
     te.wait_ge(T.sem.lq, 16 if is_root else _n(topo, root, core))
-    te.wait_ge(T.sem.ldk, 16)
 
-    def stage_a(gi):
-        n = len(groups[gi])
-        c0, c1 = span(gi)
-        S = Sb[gi % 2]
-        hn = n // 2
-        te.wait_ge(T.sem["ak%d" % gi], arrive(gi))
-        if gi >= 2:
-            need("te", t_exp[(gi - 2, len(groups[gi - 2]) - 1)])
+    def stage_a(x):
+        S = Sb[x]
         tm = []
-        for half, (lo, hi) in enumerate(((0, hn), (hn, n))):
-            tm.append(post(te.matmul(S[half][:, 0:128 * (hi - lo)], T.qs[:, h * 128:(h + 1) * 128],
-                                     T.Kall[:, c0 + lo * 128:c0 + hi * 128], True, True), "te"))
-        for half, (lo, hi) in enumerate(((0, hn), (hn, n))):
+        for half in (0, 1):
+            if x == 0:
+                te.wait_ge(T.sem["ak%d" % half], arrive(grp[half * hn:(half + 1) * hn]))
+            tm.append(post(te.matmul(S[half][:, 0:128 * hn], T.qs[:, x * 128:(x + 1) * 128],
+                                     T.Kall[:, half * hn * 128:(half + 1) * hn * 128], True, True), "te"))
+        mb = cols(4)
+        for half in (0, 1):
             need("ve", tm[half])
-            t = post(ve.tensor_reduce(mcol[:, 3 * gi + 1 + half:3 * gi + 2 + half], S[half][:, 0:128 * (hi - lo)],
-                                      AxisListType.X, AluOpType.max, negate=True), "ve")
+            t = post(ve.tensor_reduce(mb[:, 1 + half:2 + half], S[half][:, 0:128 * hn], AxisListType.X, AluOpType.max,
+                                      negate=True), "ve")
+        if is_root:
+            ve.wait_ge(T.sem["am%d" % x], n_pk)
+            t = post(ve.tensor_reduce(mb[:, 0:1], ml[x][:, 0:2], AxisListType.X, AluOpType.min), "ve")
         need("ve", t)
-        nm = mcol[:, 3 * gi + 3:3 * gi + 4]
-        t = post(ve.tensor_reduce(nm, mcol[:, (3 * gi if gi > 0 else 1):3 * gi + 3], AxisListType.X, AluOpType.min),
+        t = post(ve.tensor_reduce(mb[:, 3:4], mb[:, 0:3] if is_root else mb[:, 1:3], AxisListType.X, AluOpType.min),
                  "ve")
-        negM[gi] = nm
+        negM[x], t_M[x] = mb[:, 3:4], t
         need("se", t)
-        lblk[gi] = cols(n)
         for i in range(n):
-            t_exp[(gi, i)] = post(se.activation(T.P[:, c0 + i * 128:c0 + (i + 1) * 128],
-                                                S[i // hn][:, (i % hn) * 128:(i % hn + 1) * 128],
-                                                Exp, bias=negM[gi], scale=1.0, accum_out=lblk[gi][:, i:i + 1]), "se")
-        if gi > 0:
-            a[gi] = cols()
-            t_a[gi] = post(se.activation(a[gi], negM[gi - 1], Exp, bias=negM[gi], scale=-1.0), "se")
+            t_exp[(x, i)] = post(se.activation(T.P[:, (x * n + i) * 128:(x * n + i + 1) * 128],
+                                               S[i // hn][:, (i % hn) * 128:(i % hn + 1) * 128],
+                                               Exp, bias=negM[x], scale=1.0), "se")
+        if is_root:
+            se.wait_ge(T.sem["am%d" % x], n_pk)
+            bc[x] = cols(2)
+            t_b[x] = post(se.activation(bc[x], ml[x][:, 0:2], Exp, bias=negM[x], scale=-1.0), "se")
 
-    def stage_b(gi):
-        n = len(groups[gi])
-        c0, c1 = span(gi)
-        if gi > 0:
-            need("se", t_a[gi])
-            need("se", t_acc[gi - 1])
-            t_sc[gi] = post(se.activation(T.acc[:, :], T.acc[:, :], Copy, scale=a[gi]), "se")
+    def stage_t(x):
         need("te", t_id)
         for half in (0, 1):
-            lo, hi = half * (n // 2), (n // 2 if half == 0 else n)
-            need("te", t_cp.get((gi - 1, half)))
+            lo, hi = half * hn, (half + 1) * hn
+            need("te", t_cp.get((x - 1, half)))
             for i in range(lo, hi):
-                need("te", t_exp[(gi, i)])
+                need("te", t_exp[(x, i)])
                 t = post(te.transpose(Tb[half][:, (i - lo) * 128:(i - lo + 1) * 128],
-                                      T.P[:, c0 + i * 128:c0 + (i + 1) * 128], T.ident[:, :]), "te")
+                                      T.P[:, (x * n + i) * 128:(x * n + i + 1) * 128], T.ident[:, :]), "te")
             need("ve", t)
-            t_cp[(gi, half)] = post(ve.tensor_copy(T.PT[:, c0 + lo * 128:c0 + hi * 128],
-                                                   Tb[half][:, 0:(hi - lo) * 128]), "ve")
-        need("ve", t_exp[(gi, n - 1)])
-        ls = cols()
-        t_l = post(ve.tensor_reduce(ls, lblk[gi], AxisListType.X, AluOpType.add), "ve")
-        if gi == 0:
-            lacc[gi] = ls
-        else:
-            need("ve", t_a[gi])
-            need("ve", t_l)
-            lacc[gi] = cols()
-            t_l = post(ve.tensor_scalar(lacc[gi], lacc[gi - 1], a[gi], ls, AluOpType.mult, AluOpType.add), "ve")
-        if gi == last:
-            need("ve", t_l)
-            rc[0] = cols()
-            t_r[0] = post(ve.reciprocal(rc[0], lacc[gi]), "ve")
+            t_cp[(x, half)] = post(ve.tensor_copy(T.PT[:, (x * n + lo) * 128:(x * n + hi) * 128],
+                                                  Tb[half][:, 0:(hi - lo) * 128]), "ve")
+        if is_root:
+            need("ve", t_id)
+            need("ve", t_b[x])
+            for v in (0, 1):
+                t_dg[x] = post(ve.tensor_scalar(T.dg[:, (2 * x + v) * 128:(2 * x + v + 1) * 128], T.ident[:, :],
+                                                bc[x][:, v:v + 1], None, AluOpType.mult), "ve")
 
-    def stage_c(gi):
-        n = len(groups[gi])
-        c0, c1 = span(gi)
-        if gi == 0:
-            te.wait_ge(T.sem.ldv, 16)
-        te.wait_ge(T.sem["av%d" % gi], arrive(gi))
-        need("te", t_acc.get(gi - 1))
+    def stage_pv(x):
+        if x == 0:
+            te.wait_ge(T.sem.av, arrive(grp))
+            need("te", t_vo)
         for i in range(n):
-            need("te", t_cp[(gi, 0 if i < n // 2 else 1)])
-            ins = te.matmul(T.O0[:, 0:128], T.PT[:, c0 + i * 128:c0 + (i + 1) * 128],
-                            T.Vall[:, c0 + i * 128:c0 + (i + 1) * 128], i == 0, i == n - 1)
-        need("ve", post(ins, "te"))
-        if gi == 0:
-            t_acc[gi] = post(ve.tensor_copy(T.acc[:, :], T.O0[:, 0:128]), "ve")
-        else:
-            need("ve", t_sc[gi])
-            t_acc[gi] = post(ve.tensor_tensor(T.acc[:, :], T.O0[:, 0:128], T.acc[:, :], AluOpType.add), "ve")
+            need("te", t_cp[(x, 0 if i < hn else 1)])
+            ins = te.matmul(Ob[x][:, 0:129], T.PT[:, (x * n + i) * 128:(x * n + i + 1) * 128],
+                            T.Vall[:, i * VS:i * VS + 129], i == 0, (not is_root) and i == n - 1)
+        if not is_root:
+            need("ve", post(ins, "te"))
+            t_o[x] = post(ve.tensor_copy(T.pk[:, x * VS:x * VS + 129], Ob[x][:, 0:129]), "ve")
+
+    def stage_mg(x):
+        te.wait_ge(T.sem["ap%d" % x], n_pk)
+        need("te", t_dg[x])
+        for v in (0, 1):
+            ins = te.matmul(Ob[x][:, 0:129], T.dg[:, (2 * x + v) * 128:(2 * x + v + 1) * 128],
+                            T.pkl[:, (2 * x + v) * VS:(2 * x + v) * VS + 129], False, v == 1)
+        t_o[x] = post(ins, "te")
+
+    def final(x):
+        need("ve", t_o[x])
+        rc = cols()
+        need("ve", post(ve.reciprocal(rc, Ob[x][:, 128:129]), "ve"))
+        t = post(ve.tensor_scalar(T.ysb[:, x * 128:(x + 1) * 128], Ob[x][:, 0:128], rc, None, AluOpType.mult), "ve")
+        q = "sy" if x == 0 else "se"
+        need(q, t)
+        queues[q].dma_start(T.y[x * 128:(x + 1) * 128, :], T.ysb[:, x * 128:(x + 1) * 128]).then_inc(
+            T.sem["yd%d" % x], 16)
 
     stage_a(0)
-    for gi in range(len(groups)):
-        if gi < last:
-            stage_a(gi + 1)
-        stage_b(gi)
-        stage_c(gi)
-    need("ve", t_acc[last])
-    need("ve", t_r[0])
-    t_y = post(ve.tensor_scalar(T.ysb[:, :], T.acc[:, :], rc[0], None, AluOpType.mult), "ve")
+    stage_a(1)
+    stage_t(0)
+    stage_pv(0)
+    stage_t(1)
     if is_root:
-        need("sy", t_y)
-        g.sync.dma_start(T.y[0:128, :], T.ysb[:, :]).then_inc(T.sem.yd0, 16)
-        se.wait_ge(T.sem.yar, _n(topo, hub, root))
-        se.dma_start(T.y[128:256, :], T.yland[:, :]).then_inc(T.sem.yd1, 16)
+        stage_mg(0)
+        stage_pv(1)
+        stage_mg(1)
+        final(0)
+        final(1)
     else:
-        need("ge", t_y)
-        sent += _send(g, T, topo, core, root, T.yland[:, :], T.ysb[:, :], T.sem.yar)
+        stage_pv(1)
+        for x in (0, 1):
+            need("ge", t_M[x])
+            sent += _send(g, T, topo, core, root, ml[x][:, w:w + 1], negM[x], T.sem["am%d" % x])
+        for x in (0, 1):
+            need("ge", t_o[x])
+            sent += _send(g, T, topo, core, root, T.pkl[:, (2 * x + w) * VS:(2 * x + w) * VS + 129],
+                          T.pk[:, x * VS:x * VS + 129], T.sem["ap%d" % x])
     for e in ("te", "ve", "se", "ge"):
         g.wait_ge(T.sem[e], cnt[e])
     g.wait_ge(T.sem.sent, sent)
@@ -306,7 +316,7 @@ def rank_program(g, core, T, topo):
     if rank is None:
         return
     plan = _plan(T, topo)
-    if core == plan[1] or core == plan[2]:
+    if core in plan[2]:
         _worker(g, core, T, topo, rank, plan)
     else:
         _sender(g, core, T, topo, rank, plan)

from concourse.bass import DstId, RemoteDMATransfer
from concourse.mybir import AluOpType, AxisListType, ActivationFunctionType

VS = 136

SCRATCH = {
    "kd": ("dram", [128, 128], "bfloat16"),
    "vd": ("dram", [128, 128], "bfloat16"),
    "rk": ("dram", [128, 128], "bfloat16"),
    "rv": ("dram", [128, 128], "bfloat16"),
    "qs": ("sbuf", [128, 256], "bfloat16"),
    "ks": ("sbuf", [128, 128], "bfloat16"),
    "vs": ("sbuf", [128, 128], "bfloat16"),
    "Kall": ("sbuf", [128, 4 * 128], "bfloat16"),
    "Vall": ("sbuf", [128, 4 * VS], "bfloat16"),
    "zer": ("sbuf", [128, 128], "bfloat16"),
    "ones": ("sbuf", [128, 128], "bfloat16"),
    "ident": ("sbuf", [128, 128], "bfloat16"),
    "P": ("sbuf", [128, 8 * 128], "bfloat16"),
    "PT": ("sbuf", [128, 8 * 128], "bfloat16"),
    "st": ("sbuf", [128, 32], "float32"),
    "pk": ("sbuf", [128, 2 * VS], "bfloat16"),
    "pkl": ("sbuf", [128, 4 * VS], "bfloat16"),
    "ml0": ("sbuf", [128, 2], "float32"),
    "ml1": ("sbuf", [128, 2], "float32"),
    "dg": ("sbuf", [128, 4 * 128], "bfloat16"),
    "ysb": ("sbuf", [128, 256], "bfloat16"),
    "S0a": ("psum", [128, 512], "float32"),
    "S0b": ("psum", [128, 512], "float32"),
    "S1a": ("psum", [128, 512], "float32"),
    "S1b": ("psum", [128, 512], "float32"),
    "TA": ("psum", [128, 1024], "bfloat16"),
    "TB": ("psum", [128, 1024], "bfloat16"),
    "O0": ("psum", [128, 512], "float32"),
    "O1": ("psum", [128, 512], "float32"),
}
SEMAPHORES = ["ldk", "ldv", "rka", "rva", "sent", "lq", "yd0", "yd1", "te", "ve", "se", "ge", "ak0", "ak1", "av",
              "am0", "am1", "ap0", "ap1"]


def _bits(m):
    return bin(m).count("1")


def _lowest(m, n):
    n = min(n, _bits(m))
    out, b = 0, 1
    while n > 0:
        if m & b:
            out |= b
            n -= 1
        b <<= 1
    return out


def _plan(T, topo):
    cores = list(T.cores)
    root = cores[T.root]
    near = [r for r, c in enumerate(cores) if c != root and topo.chip(c) == topo.chip(root)]
    near.sort(key=lambda r: 0 if topo.die(cores[r]) == topo.die(root) else 1)
    far = [r for r, c in enumerate(cores) if topo.chip(c) != topo.chip(root)]
    direct = [r for r in far if topo.may_write(cores[r], root)]
    passed = [r for r in far if not topo.may_write(cores[r], root)]
    via = {}
    for r in passed:
        c = cores[r]
        cand = [d for d in direct if topo.chip(cores[d]) == topo.chip(c)]
        same = [d for d in cand if topo.die(cores[d]) == topo.die(c)]
        cand = same + [d for d in cand if d not in same]
        free = [d for d in cand if d not in via.values()]
        via[r] = (free or cand)[0]
    groups = [[near[1], near[2], T.root, direct[0]], [near[0]] + direct[1:], passed]
    W = [cores[near[0]], cores[near[1]], root]
    place = {}
    for w, grp in enumerate(groups):
        for s, r in enumerate(grp):
            place[r] = (W[w], s)
    return cores, root, W, groups, place, via


NE = 8


def _n(topo, src, dst):
    return _bits(_lowest(topo.mask(src, dst), NE))


def _send(g, T, topo, src, dst, out_ap, in_ap, rsem):
    rid, pid, _ = topo.addr(dst)
    g.remote_dma(out_ap=out_ap, in_ap=in_ap, remote_sem=rsem, local_sem=T.sem.sent, pid=pid, routing_id=rid,
                 dma_engine_mask=_lowest(topo.mask(src, dst), NE))
    return _n(topo, src, dst)


def _kslot(T, s):
    return T.Kall[:, s * 128:(s + 1) * 128]


def _vslot(T, s):
    return T.Vall[:, s * VS:s * VS + 128]


def _ksem(T, s):
    return T.sem["ak%d" % (s // 2)]


def _sender(g, core, T, topo, rank, plan):
    cores, root, W, groups, place, via = plan
    g.sync.dma_start(T.kd[:, :], T.k[:, :]).then_inc(T.sem.ldk, 16)
    g.scalar.dma_start(T.vd[:, :], T.v[:, :]).then_inc(T.sem.ldv, 16)
    sent = 0
    if rank in via:
        dst = cores[via[rank]]
        g.wait_ge(T.sem.ldk, 16)
        sent += _send(g, T, topo, core, dst, T.rk[:, :], T.kd[:, :], T.sem.rka)
        g.wait_ge(T.sem.ldv, 16)
        sent += _send(g, T, topo, core, dst, T.rv[:, :], T.vd[:, :], T.sem.rva)
    else:
        dst, s = place[rank]
        g.wait_ge(T.sem.ldk, 16)
        sent += _send(g, T, topo, core, dst, _kslot(T, s), T.kd[:, :], _ksem(T, s))
        g.wait_ge(T.sem.ldv, 16)
        sent += _send(g, T, topo, core, dst, _vslot(T, s), T.vd[:, :], T.sem.av)
        for r in [r for r in via if via[r] == rank]:
            dst, s = place[r]
            g.wait_ge(T.sem.rka, _n(topo, cores[r], core))
            sent += _send(g, T, topo, core, dst, _kslot(T, s), T.rk[:, :], _ksem(T, s))
            g.wait_ge(T.sem.rva, _n(topo, cores[r], core))
            sent += _send(g, T, topo, core, dst, _vslot(T, s), T.rv[:, :], T.sem.av)
    g.wait_ge(T.sem.sent, sent)


def _worker(g, core, T, topo, rank, plan):
    cores, root, W, groups, place, via = plan
    is_root = core == root
    w = W.index(core)
    grp = groups[w]
    n = len(grp)
    hn = n // 2
    te, ve, se = g.tensor, g.vector, g.scalar
    Exp = ActivationFunctionType.Exp
    cnt = {"te": 0, "ve": 0, "se": 0, "ge": 0}
    seen = {}
    queues = {"te": te, "ve": ve, "se": se, "ge": g, "sy": g.sync}

    def post(ins, e):
        cnt[e] += 1
        ins.then_inc(T.sem[e], 1)
        return (e, cnt[e])

    def need(q, tok):
        if tok is None:
            return
        e, m = tok
        if seen.get((q, e), 0) >= m:
            return
        seen[(q, e)] = m
        queues[q].wait_ge(T.sem[e], m)

    ncol = [0]

    def cols(m=1):
        c = ncol[0]
        ncol[0] += m
        return T.st[:, c:c + m]

    if is_root:
        g.sync.dma_start(T.qs[:, :], T.q[:, :]).then_inc(T.sem.lq, 16)
    g.scalar.dma_start(T.ks[:, :], T.k[:, :]).then_inc(T.sem.ldk, 16)
    g.sync.dma_start(T.vs[:, :], T.v[:, :]).then_inc(T.sem.ldv, 16)
    need("se", post(ve.memset(T.zer[:, :], 0.0), "ve"))
    t_ones = post(se.activation(T.ones[:, :], T.zer[:, :], Exp), "se")
    for s in range(n):
        t_vo = post(ve.memset(T.Vall[:, s * VS + 128:(s + 1) * VS], 1.0), "ve")
    sent = 0
    if is_root:
        g.wait_ge(T.sem.lq, 16)
        trs, used = [], 0
        for d in W[:2]:
            rid, pid, _ = topo.addr(d)
            m = _lowest(topo.mask(core, d) & ~used, NE)
            used |= m
            trs.append(RemoteDMATransfer(dst_ids=[DstId(rid=rid, pnc=pid)], dma_engine_mask=m, remote_sem=T.sem.lq,
                                         src=T.qs[:, :], dst=T.qs[:, :]))
            sent += _bits(m)
        g.remote_dma_fused(trs, local_sem=T.sem.sent)
    dst, s = place[rank]
    g.wait_ge(T.sem.ldk, 16)
    sent += _send(g, T, topo, core, dst, _kslot(T, s), T.ks[:, :], _ksem(T, s))
    g.wait_ge(T.sem.ldv, 16)
    sent += _send(g, T, topo, core, dst, _vslot(T, s), T.vs[:, :], T.sem.av)
    need("ge", t_ones)
    t_id = post(g.affine_select(T.ident[:, :], T.ones[:, :], [[-1, 128]], AluOpType.is_equal, 0.0, 0, 1), "ge")

    def arrive(rs):
        return sum(_n(topo, cores[via[r]] if r in via else cores[r], core) for r in rs)

    n_pk = sum(_n(topo, d, root) for d in W[:2])
    Sb = [[T.S0a, T.S0b], [T.S1a, T.S1b]]
    Tb = [T.TA, T.TB]
    Ob = [T.O0, T.O1]
    ml = [T.ml0, T.ml1]
    t_exp, t_cp, t_M, t_b, t_dg, t_o = {}, {}, {}, {}, {}, {}
    negM, bc = {}, {}
    te.wait_ge(T.sem.lq, 16 if is_root else _n(topo, root, core))

    def stage_a(x):
        S = Sb[x]
        tm = []
        for half in (0, 1):
            if x == 0:
                te.wait_ge(T.sem["ak%d" % half], arrive(grp[half * hn:(half + 1) * hn]))
            tm.append(post(te.matmul(S[half][:, 0:128 * hn], T.qs[:, x * 128:(x + 1) * 128],
                                     T.Kall[:, half * hn * 128:(half + 1) * hn * 128], True, True), "te"))
        mb = cols(4)
        for half in (0, 1):
            need("ve", tm[half])
            t = post(ve.tensor_reduce(mb[:, 1 + half:2 + half], S[half][:, 0:128 * hn], AxisListType.X, AluOpType.max,
                                      negate=True), "ve")
        if is_root:
            ve.wait_ge(T.sem["am%d" % x], n_pk)
            t = post(ve.tensor_reduce(mb[:, 0:1], ml[x][:, 0:2], AxisListType.X, AluOpType.min), "ve")
        need("ve", t)
        t = post(ve.tensor_reduce(mb[:, 3:4], mb[:, 0:3] if is_root else mb[:, 1:3], AxisListType.X, AluOpType.min),
                 "ve")
        negM[x], t_M[x] = mb[:, 3:4], t
        need("se", t)
        for i in range(n):
            t_exp[(x, i)] = post(se.activation(T.P[:, (x * n + i) * 128:(x * n + i + 1) * 128],
                                               S[i // hn][:, (i % hn) * 128:(i % hn + 1) * 128],
                                               Exp, bias=negM[x], scale=1.0), "se")
        if is_root:
            se.wait_ge(T.sem["am%d" % x], n_pk)
            bc[x] = cols(2)
            t_b[x] = post(se.activation(bc[x], ml[x][:, 0:2], Exp, bias=negM[x], scale=-1.0), "se")

    def stage_t(x):
        need("te", t_id)
        for half in (0, 1):
            lo, hi = half * hn, (half + 1) * hn
            need("te", t_cp.get((x - 1, half)))
            for i in range(lo, hi):
                need("te", t_exp[(x, i)])
                t = post(te.transpose(Tb[half][:, (i - lo) * 128:(i - lo + 1) * 128],
                                      T.P[:, (x * n + i) * 128:(x * n + i + 1) * 128], T.ident[:, :]), "te")
            need("ve", t)
            t_cp[(x, half)] = post(ve.tensor_copy(T.PT[:, (x * n + lo) * 128:(x * n + hi) * 128],
                                                  Tb[half][:, 0:(hi - lo) * 128]), "ve")
        if is_root:
            need("ve", t_id)
            need("ve", t_b[x])
            for v in (0, 1):
                t_dg[x] = post(ve.tensor_scalar(T.dg[:, (2 * x + v) * 128:(2 * x + v + 1) * 128], T.ident[:, :],
                                                bc[x][:, v:v + 1], None, AluOpType.mult), "ve")

    def stage_pv(x):
        if x == 0:
            te.wait_ge(T.sem.av, arrive(grp))
            need("te", t_vo)
        for i in range(n):
            need("te", t_cp[(x, 0 if i < hn else 1)])
            ins = te.matmul(Ob[x][:, 0:129], T.PT[:, (x * n + i) * 128:(x * n + i + 1) * 128],
                            T.Vall[:, i * VS:i * VS + 129], i == 0, (not is_root) and i == n - 1)
        if not is_root:
            need("ve", post(ins, "te"))
            t_o[x] = post(ve.tensor_copy(T.pk[:, x * VS:x * VS + 129], Ob[x][:, 0:129]), "ve")

    def stage_mg(x):
        te.wait_ge(T.sem["ap%d" % x], n_pk)
        need("te", t_dg[x])
        for v in (0, 1):
            ins = te.matmul(Ob[x][:, 0:129], T.dg[:, (2 * x + v) * 128:(2 * x + v + 1) * 128],
                            T.pkl[:, (2 * x + v) * VS:(2 * x + v) * VS + 129], False, v == 1)
        t_o[x] = post(ins, "te")

    def final(x):
        need("ve", t_o[x])
        rc = cols()
        need("ve", post(ve.reciprocal(rc, Ob[x][:, 128:129]), "ve"))
        t = post(ve.tensor_scalar(T.ysb[:, x * 128:(x + 1) * 128], Ob[x][:, 0:128], rc, None, AluOpType.mult), "ve")
        q = "sy" if x == 0 else "se"
        need(q, t)
        queues[q].dma_start(T.y[x * 128:(x + 1) * 128, :], T.ysb[:, x * 128:(x + 1) * 128]).then_inc(
            T.sem["yd%d" % x], 16)

    stage_a(0)
    stage_a(1)
    stage_t(0)
    stage_pv(0)
    stage_t(1)
    if is_root:
        stage_mg(0)
        stage_pv(1)
        stage_mg(1)
        final(0)
        final(1)
    else:
        stage_pv(1)
        for x in (0, 1):
            need("ge", t_M[x])
            sent += _send(g, T, topo, core, root, ml[x][:, w:w + 1], negM[x], T.sem["am%d" % x])
        for x in (0, 1):
            need("ge", t_o[x])
            sent += _send(g, T, topo, core, root, T.pkl[:, (2 * x + w) * VS:(2 * x + w) * VS + 129],
                          T.pk[:, x * VS:x * VS + 129], T.sem["ap%d" % x])
    for e in ("te", "ve", "se", "ge"):
        g.wait_ge(T.sem[e], cnt[e])
    g.wait_ge(T.sem.sent, sent)
    if is_root:
        g.wait_ge(T.sem.yd0, 16)
        g.wait_ge(T.sem.yd1, 16)


def rank_program(g, core, T, topo):
    rank = T.rank_of(core)
    if rank is None:
        return
    plan = _plan(T, topo)
    if core in plan[2]:
        _worker(g, core, T, topo, rank, plan)
    else:
        _sender(g, core, T, topo, rank, plan)
